import numpy as np
import ml_dtypes


def mxq(x, axis, fmt="e4m3"):
    dtype, down = {"e4m3": (ml_dtypes.float8_e4m3fn, 7), "e5m2": (ml_dtypes.float8_e5m2, 14)}[fmt]
    v = np.moveaxis(np.asarray(x, np.float32).astype(ml_dtypes.bfloat16).astype(np.float64), axis, -1)
    blocks = v.reshape(v.shape[:-1] + (-1, 32))
    amax = np.abs(blocks).max(-1, keepdims=True)
    byte = np.maximum(np.where(amax > 0, np.frexp(amax)[1] - 1 + 127, 0) - down, 1)
    scale = np.exp2(byte - 127.0)
    codes = (blocks / scale).astype(np.float32).astype(dtype).astype(np.float64)
    return np.moveaxis((codes * scale).reshape(v.shape), -1, axis)


WIDE = False


def mx_kscale(k):
    if not WIDE:
        return np.ones(k)
    levels = np.array([10, -10, 5, -5, 0])
    if k % 512:
        return np.exp2(np.random.permutation(np.resize(levels, k // 32))).repeat(32)
    a = np.empty((k // 512, 16))
    for p in range(k // 512):
        a[p, :8] = np.random.permutation(np.resize(levels, 8))
        for g in range(8):
            far = levels[np.abs(levels - a[p, g]) >= 10]
            a[p, g + 8] = far[np.random.randint(len(far))]
    return np.exp2(a.ravel()).repeat(32)


def f64(x):
    return np.asarray(x).astype(np.float64)


def striped(idx):
    return np.tile(idx.reshape(-1, 16).T, (8, 1)).astype(np.uint16)


def unstriped(offs):
    return offs[:16].T.reshape(-1).astype(np.int64)


def pack_weight(w):
    k, n = w.shape
    w = f64(np.asarray(w, np.float32).astype(ml_dtypes.bfloat16)).reshape(k // 32, 32, n)
    amax = np.abs(w).max(1)
    byte = np.clip(np.where(amax > 0, np.frexp(amax)[1] - 1 + 127 - 7, 1), 1, 254)
    scaled = (w * np.exp2(127.0 - byte)[:, None, :]).reshape(k, n).astype(np.float32)
    words = np.ascontiguousarray(scaled.reshape(k // 512, 128, 4, n).transpose(0, 1, 3, 2)).astype(ml_dtypes.float8_e4m3fn).view(np.uint8)
    return words, np.ascontiguousarray(byte.astype(np.uint8).reshape(k // 512, 16, n))


def unpack_weight(words, scales):
    g, p, n, _ = words.shape
    vals = np.ascontiguousarray(words).view(ml_dtypes.float8_e4m3fn).astype(np.float64) * np.repeat(np.exp2(scales.astype(np.float64) - 127.0), 8, axis=1)[..., None]
    return vals.transpose(0, 1, 3, 2).reshape(g * 512, n)


K, T, S, N, V, U = 1024, 1024, 512, 256, 256, 512
P = 2 ** 7


def setup_inputs():
    n = np.random.standard_normal
    s = mx_kscale(K)[:, None]
    packed_xT = pack_weight(n((K, T)) * s)
    return {
        "x_words": packed_xT[0],
        "x_scales": packed_xT[1],
        "w1": (n((K, N)) / np.sqrt(K) / s).astype(np.float32),
        "kern": (np.tile(np.random.uniform(0.1, 0.8, U), (P, 1))).astype(np.float32),
        "sink": (np.random.uniform(0.2, 1.0, (N, 1))).astype(np.float32),
        "offs": striped(np.random.permutation(T)[:S]),
        "ba": striped(np.random.permutation(S)),
        "bb": striped(np.random.permutation(S)),
        "gaina": striped(np.random.permutation(U)[:V]),
        "gainb": striped(np.random.permutation(U)[:V]),
        "lossa": striped(np.random.permutation(U)[:V]),
        "who": striped(np.random.permutation(S)[:V]),
    }


def reference(x_words, x_scales, w1, kern, sink, offs, ba, bb, gaina, gainb, lossa, who):
    xq = unpack_weight(x_words, x_scales)[:, unstriped(offs)]
    y = mxq(f64(w1), 0, "e4m3").T @ xq
    num = np.exp(0.6 * y)
    rate = (f64(kern)[:1] * num[:, unstriped(ba)]) * num[:, unstriped(bb)]
    gain = 0.5 * (rate[:, unstriped(gaina)] + rate[:, unstriped(gainb)])
    own = num[:, unstriped(who)]
    return np.log(gain + 0.1) - (f64(sink) * (rate[:, unstriped(lossa)] / (own + 0.2)))

@@ -1,0 +1,151 @@
+import math
+from contextlib import ExitStack
+
+import concourse.mybir as mybir
+
+K, T, S, N, V = 1024, 1024, 512, 256, 256
+FLOPS = 2 * K * N * S
+
+F32 = mybir.dt.float32
+BF16 = mybir.dt.bfloat16
+I32 = mybir.dt.int32
+U32 = mybir.dt.uint32
+U16 = mybir.dt.uint16
+U8 = mybir.dt.uint8
+FP8X4 = mybir.dt.float8_e4m3fn_x4
+ACT = mybir.ActivationFunctionType
+MULT = mybir.AluOpType.mult
+ADD = mybir.AluOpType.add
+
+P = 128
+PACK = 4
+PASSES = K // (P * PACK)
+BLOCKS = N // P
+HALF = S // 2
+LIST_ROWS = 16
+
+
+def tile_picked_ycoagu_log_p_kernel(tc, x_words, x_scales, w1, kern, sink, offs, ba, bb, gaina, gainb, lossa, who, out):
+    nc = tc.nc
+    with ExitStack() as ctx:
+        pool = ctx.enter_context(tc.tile_pool(name="sbuf", bufs=1))
+        psum = ctx.enter_context(tc.psum_pool(name="psum", bufs=1))
+
+        def load_list(name, src):
+            t = pool.tile(list(src.shape), U16, name=name)
+            nc.sync.dma_start(t[:], src)
+            return t
+
+        def half_of(lst, h):
+            cols = HALF // LIST_ROWS
+            return lst[:, h * cols:(h + 1) * cols]
+
+        w_view = w1.rearrange("(o p t) n -> o p t n", p=P, t=PACK)
+
+        def load_w(b):
+            raw = []
+            for o in range(PASSES):
+                t = pool.tile([P, PACK, P], F32, name="w_raw%d%d" % (b, o))
+                nc.sync.dma_start(t[:], w_view[o][:, :, b * P:(b + 1) * P])
+                raw.append(t)
+            return raw
+
+        offs_t = load_list("offs_t", offs)
+        xs = pool.tile([P, T], U8, name="xs")
+        nc.gpsimd.memset(xs[:].bitcast(I32), 0)
+        for q in range(4):
+            nc.scalar.dma_start(xs[32 * q:32 * q + 4 * PASSES, :].bitcast(I32), x_scales[:, 4 * q:4 * q + 4, :].bitcast(I32))
+        w_raw = [load_w(0)]
+        xw = []
+        for o in range(PASSES):
+            t = pool.tile([P, T], I32, name="xw%d" % o)
+            nc.sync.dma_start(t[:], x_words[o].rearrange("p n t -> p (n t)").bitcast(I32))
+            xw.append(t)
+        w_raw.append(load_w(1))
+        ba_t = load_list("ba_t", ba)
+        bb_t = load_list("bb_t", bb)
+        kern_t = pool.tile([P, S], F32, name="kern_t")
+        nc.sync.dma_start(kern_t[:], kern)
+        who_t = load_list("who_t", who)
+        gaina_t = load_list("gaina_t", gaina)
+        gainb_t = load_list("gainb_t", gainb)
+        lossa_t = load_list("lossa_t", lossa)
+        sink_t = pool.tile([P, BLOCKS], F32, name="sink_t")
+        with nc.allow_non_contiguous_dma(reason="one value a row"):
+            nc.sync.dma_start(sink_t[:], sink.rearrange("(b p) o -> p (b o)", p=P))
+        loss_w = pool.tile([P, BLOCKS], F32, name="loss_w")
+        nc.gpsimd.tensor_scalar(loss_w[:], sink_t[:], -5.0, 0.0, MULT, ADD)
+
+        def quantize_w(b, copy):
+            grouped = pool.tile([P, PASSES * P * PACK], BF16, name="w_grouped%d" % b, align_bytes=64)
+            for o in range(PASSES):
+                dst = grouped[:, o * P * PACK:(o + 1) * P * PACK]
+                copy(dst.rearrange("p (c i t) -> p c t i", i=4, t=PACK),
+                     w_raw[b][o][:].rearrange("p t (c i) -> p c t i", i=4))
+            codes = pool.tile([P, PASSES * P], U32, name="w_codes%d" % b, align_bytes=64)
+            scales = pool.tile([P, PASSES * P], U8, name="w_scales%d" % b, align_bytes=64)
+            nc.vector.quantize_mx(out=codes[:].bitcast(FP8X4), scales=scales[:], in_=grouped[:])
+            return codes, scales
+
+        xs_g = pool.tile([P, S], U8, name="xs_g", align_bytes=64)
+        nc.vector.tensor_copy(xs_g[:], xs[:].indirect(offs_t[:]))
+        wq = [quantize_w(0, nc.scalar.copy)]
+        xw_g = [pool.tile([P, S], U32, name="xw_g%d" % o, align_bytes=64) for o in range(PASSES)]
+        nc.vector.tensor_copy(xw_g[0][:], xw[0][:].bitcast(U32).indirect(offs_t[:]))
+        for h in range(2):
+            nc.vector.tensor_copy(xw_g[1][:, h * HALF:(h + 1) * HALF], xw[1][:].bitcast(U32).indirect(half_of(offs_t, h)))
+        wq.append(quantize_w(1, nc.vector.tensor_copy))
+
+        def product(b, cols, name):
+            acc = psum.tile([P, cols.stop - cols.start], F32, name=name)
+            codes, scales = wq[b]
+            for o in range(PASSES):
+                nc.tensor.matmul_mx(
+                    out=acc[:],
+                    lhsT=codes[:, o * P:(o + 1) * P].bitcast(FP8X4),
+                    lhsT_scale=scales[:, o * P:(o + 1) * P],
+                    rhs=xw_g[o][:, cols].bitcast(FP8X4),
+                    rhs_scale=xs_g[4 * o:, cols],
+                    start=(o == 0), stop=(o == PASSES - 1))
+            return acc
+
+        pieces = [[slice(0, HALF), slice(HALF, S)], [slice(0, S)]]
+        y = [[product(b, c, "y%d_%d" % (b, c.start)) for c in pieces[b]] for b in range(BLOCKS)]
+        num = [pool.tile([P, S], F32, name="num%d" % b) for b in range(BLOCKS)]
+        z = [pool.tile([P, S], F32, name="z%d" % b) for b in range(BLOCKS)]
+        for b in range(BLOCKS):
+            for c, acc in zip(pieces[b], y[b]):
+                nc.scalar.activation(num[b][:, c], acc[:], ACT.Exp, scale=0.6)
+        for b in range(BLOCKS):
+            for c, acc in zip(pieces[b], y[b]):
+                nc.scalar.activation(z[b][:, c], acc[:], ACT.Copy, scale=-0.6, bias=-math.log(5.0))
+        inv = [pool.tile([P, V], F32, name="inv%d" % b) for b in range(BLOCKS)]
+        for b in range(BLOCKS):
+            nc.scalar.activation(inv[b][:], z[b][:].indirect(who_t[:]), ACT.Sigmoid)
+
+        rate = []
+        for b in range(BLOCKS):
+            part = pool.tile([P, S], F32, name="part%d" % b)
+            r = pool.tile([P, S], F32, name="rate%d" % b)
+            for h in range(2):
+                c = slice(h * HALF, (h + 1) * HALF)
+                nc.vector.tensor_tensor(part[:, c], num[b][:].indirect(half_of(ba_t, h)), kern_t[:, c], MULT)
+            for h in range(2):
+                c = slice(h * HALF, (h + 1) * HALF)
+                nc.vector.tensor_tensor(r[:, c], num[b][:].indirect(half_of(bb_t, h)), part[:, c], MULT)
+            rate.append(r)
+        first = [pool.tile([P, V], F32, name="first%d" % b) for b in range(BLOCKS)]
+        both = [pool.tile([P, V], F32, name="both%d" % b) for b in range(BLOCKS)]
+        loss = [pool.tile([P, V], F32, name="loss%d" % b) for b in range(BLOCKS)]
+        logg = [pool.tile([P, V], F32, name="logg%d" % b) for b in range(BLOCKS)]
+        res = [pool.tile([P, V], F32, name="res%d" % b) for b in range(BLOCKS)]
+        for b in range(BLOCKS):
+            nc.vector.tensor_copy(first[b][:], rate[b][:].indirect(gaina_t[:]))
+        for b in range(BLOCKS):
+            nc.vector.tensor_tensor(both[b][:], rate[b][:].indirect(gainb_t[:]), first[b][:], ADD)
+            nc.scalar.activation(logg[b][:], both[b][:], ACT.Ln, scale=0.5, bias=0.1)
+        for b in range(BLOCKS):
+            nc.vector.tensor_tensor(loss[b][:], rate[b][:].indirect(lossa_t[:]), inv[b][:], MULT)
+        for b in range(BLOCKS):
+            nc.vector.scalar_tensor_tensor(res[b][:], loss[b][:], loss_w[:, b:b + 1], logg[b][:], MULT, ADD)
+            nc.sync.dma_start(out[b * P:(b + 1) * P, :], res[b][:])

@@ -23,6 +23,7 @@ PASSES = K // (P * PACK)
 BLOCKS = N // P
 HALF = S // 2
 LIST_ROWS = 16
+EXP_WINDOW = 2048
 
 
 def tile_picked_ycoagu_log_p_kernel(tc, x_words, x_scales, w1, kern, sink, offs, ba, bb, gaina, gainb, lossa, who, out):
@@ -42,26 +43,24 @@ def tile_picked_ycoagu_log_p_kernel(tc, x_words, x_scales, w1, kern, sink, offs,
 
         w_view = w1.rearrange("(o p t) n -> o p t n", p=P, t=PACK)
 
-        def load_w(b):
-            raw = []
-            for o in range(PASSES):
-                t = pool.tile([P, PACK, P], F32, name="w_raw%d%d" % (b, o))
-                nc.sync.dma_start(t[:], w_view[o][:, :, b * P:(b + 1) * P])
-                raw.append(t)
-            return raw
+        def load_w(name, o, cols):
+            t = pool.tile([P, PACK, cols.stop - cols.start], F32, name=name)
+            nc.sync.dma_start(t[:], w_view[o][:, :, cols])
+            return t
 
+        def load_x(o):
+            t = pool.tile([P, T], I32, name="xw%d" % o)
+            nc.sync.dma_start(t[:], x_words[o].rearrange("p n t -> p (n t)").bitcast(I32))
+            return t
+
+        w_raw = [load_w("w_raw0", 0, slice(0, N))]
         offs_t = load_list("offs_t", offs)
         xs = pool.tile([P, T], U8, name="xs")
         nc.gpsimd.memset(xs[:].bitcast(I32), 0)
         for q in range(4):
-            nc.scalar.dma_start(xs[32 * q:32 * q + 4 * PASSES, :].bitcast(I32), x_scales[:, 4 * q:4 * q + 4, :].bitcast(I32))
-        w_raw = [load_w(0)]
-        xw = []
-        for o in range(PASSES):
-            t = pool.tile([P, T], I32, name="xw%d" % o)
-            nc.sync.dma_start(t[:], x_words[o].rearrange("p n t -> p (n t)").bitcast(I32))
-            xw.append(t)
-        w_raw.append(load_w(1))
+            nc.sync.dma_start(xs[32 * q:32 * q + 4 * PASSES, :].bitcast(I32), x_scales[:, 4 * q:4 * q + 4, :].bitcast(I32))
+        w_raw.append(load_w("w_raw1", 1, slice(0, N)))
+        xw = [load_x(o) for o in range(PASSES)]
         ba_t = load_list("ba_t", ba)
         bb_t = load_list("bb_t", bb)
         kern_t = pool.tile([P, S], F32, name="kern_t")
@@ -76,76 +75,77 @@ def tile_picked_ycoagu_log_p_kernel(tc, x_words, x_scales, w1, kern, sink, offs,
         loss_w = pool.tile([P, BLOCKS], F32, name="loss_w")
         nc.gpsimd.tensor_scalar(loss_w[:], sink_t[:], -5.0, 0.0, MULT, ADD)
 
-        def quantize_w(b, copy):
-            grouped = pool.tile([P, PASSES * P * PACK], BF16, name="w_grouped%d" % b, align_bytes=64)
-            for o in range(PASSES):
-                dst = grouped[:, o * P * PACK:(o + 1) * P * PACK]
-                copy(dst.rearrange("p (c i t) -> p c t i", i=4, t=PACK),
-                     w_raw[b][o][:].rearrange("p t (c i) -> p c t i", i=4))
-            codes = pool.tile([P, PASSES * P], U32, name="w_codes%d" % b, align_bytes=64)
-            scales = pool.tile([P, PASSES * P], U8, name="w_scales%d" % b, align_bytes=64)
+        def quantize_w(name, raw, copy):
+            width = raw.shape[2]
+            grouped = pool.tile([P, width * PACK], BF16, name=name + "_grouped", tag=name + "_stage", align_bytes=64)
+            copy(grouped[:].rearrange("p (c i t) -> p c t i", i=4, t=PACK),
+                 raw[:].rearrange("p t (c i) -> p c t i", i=4))
+            codes = pool.tile([P, width], U32, name=name + "_codes", align_bytes=64)
+            scales = pool.tile([P, width], U8, name=name + "_scales", align_bytes=64)
             nc.vector.quantize_mx(out=codes[:].bitcast(FP8X4), scales=scales[:], in_=grouped[:])
             return codes, scales
 
         xs_g = pool.tile([P, S], U8, name="xs_g", align_bytes=64)
+        xw_g0 = pool.tile([P, S], U32, name="xw_g0", align_bytes=64)
         nc.vector.tensor_copy(xs_g[:], xs[:].indirect(offs_t[:]))
-        wq = [quantize_w(0, nc.scalar.copy)]
-        xw_g = [pool.tile([P, S], U32, name="xw_g%d" % o, align_bytes=64) for o in range(PASSES)]
-        nc.vector.tensor_copy(xw_g[0][:], xw[0][:].bitcast(U32).indirect(offs_t[:]))
-        for h in range(2):
-            nc.vector.tensor_copy(xw_g[1][:, h * HALF:(h + 1) * HALF], xw[1][:].bitcast(U32).indirect(half_of(offs_t, h)))
-        wq.append(quantize_w(1, nc.vector.tensor_copy))
+        wq = [quantize_w("w%d" % o, w_raw[o], nc.scalar.copy) for o in range(PASSES)]
+        nc.vector.tensor_copy(xw_g0[:], xw[0][:].bitcast(U32).indirect(offs_t[:]))
+        xw_g1 = []
+        for h, stage in enumerate(("w1_stage", "w0_stage")):
+            t = pool.tile([P, HALF], U32, name="xw_g1_%d" % h, tag=stage, align_bytes=64)
+            nc.vector.tensor_copy(t[:], xw[1][:].bitcast(U32).indirect(half_of(offs_t, h)))
+            xw_g1.append(t)
 
-        def product(b, cols, name):
-            acc = psum.tile([P, cols.stop - cols.start], F32, name=name)
-            codes, scales = wq[b]
-            for o in range(PASSES):
-                nc.tensor.matmul_mx(
-                    out=acc[:],
-                    lhsT=codes[:, o * P:(o + 1) * P].bitcast(FP8X4),
-                    lhsT_scale=scales[:, o * P:(o + 1) * P],
-                    rhs=xw_g[o][:, cols].bitcast(FP8X4),
-                    rhs_scale=xs_g[4 * o:, cols],
-                    start=(o == 0), stop=(o == PASSES - 1))
-            return acc
+        halves = [slice(0, HALF), slice(HALF, S)]
+        y = [[psum.tile([P, HALF], F32, name="y%d_%d" % (b, h)) for h in range(2)] for b in range(BLOCKS)]
+        for o in range(PASSES):
+            codes, scales = wq[o]
+            for h, cols in enumerate(halves):
+                words = xw_g0[:, cols] if o == 0 else xw_g1[h][:]
+                for b in range(BLOCKS):
+                    nc.tensor.matmul_mx(
+                        out=y[b][h][:],
+                        lhsT=codes[:, b * P:(b + 1) * P].bitcast(FP8X4),
+                        lhsT_scale=scales[:, b * P:(b + 1) * P],
+                        rhs=words.bitcast(FP8X4),
+                        rhs_scale=xs_g[4 * o:, cols],
+                        start=(o == 0), stop=(o == PASSES - 1))
+        num0 = pool.tile([P, S], F32, name="num0")
+        z0 = pool.tile([P, S], F32, name="z0")
+        z1 = pool.tile([P, EXP_WINDOW], F32, name="z1")
+        nc.vector.memset(z1[:, S:], 0.0)
+        for h, c in enumerate(halves):
+            nc.scalar.activation(num0[:, c], y[0][h][:], ACT.Exp, scale=0.6)
+            nc.scalar.activation(z1[:, c], y[1][h][:], ACT.Copy, scale=-0.6, bias=-math.log(5.0))
+            nc.vector.tensor_scalar(z0[:, c], y[0][h][:], -0.6, -math.log(5.0), MULT, ADD)
+        ea = pool.tile([P, S], F32, name="ea", tag="ea")
+        eb = pool.tile([P, S], F32, name="eb")
+        nc.scalar.activation(ea[:], z1[:].indirect(ba_t[:]), ACT.Exp, scale=-1.0)
+        nc.scalar.activation(eb[:], z1[:].indirect(bb_t[:]), ACT.Exp, scale=-1.0)
 
-        pieces = [[slice(0, HALF), slice(HALF, S)], [slice(0, S)]]
-        y = [[product(b, c, "y%d_%d" % (b, c.start)) for c in pieces[b]] for b in range(BLOCKS)]
-        num = [pool.tile([P, S], F32, name="num%d" % b) for b in range(BLOCKS)]
-        z = [pool.tile([P, S], F32, name="z%d" % b) for b in range(BLOCKS)]
-        for b in range(BLOCKS):
-            for c, acc in zip(pieces[b], y[b]):
-                nc.scalar.activation(num[b][:, c], acc[:], ACT.Exp, scale=0.6)
-        for b in range(BLOCKS):
-            for c, acc in zip(pieces[b], y[b]):
-                nc.scalar.activation(z[b][:, c], acc[:], ACT.Copy, scale=-0.6, bias=-math.log(5.0))
-        inv = [pool.tile([P, V], F32, name="inv%d" % b) for b in range(BLOCKS)]
-        for b in range(BLOCKS):
-            nc.scalar.activation(inv[b][:], z[b][:].indirect(who_t[:]), ACT.Sigmoid)
-
-        rate = []
-        for b in range(BLOCKS):
-            part = pool.tile([P, S], F32, name="part%d" % b)
-            r = pool.tile([P, S], F32, name="rate%d" % b)
-            for h in range(2):
-                c = slice(h * HALF, (h + 1) * HALF)
-                nc.vector.tensor_tensor(part[:, c], num[b][:].indirect(half_of(ba_t, h)), kern_t[:, c], MULT)
-            for h in range(2):
-                c = slice(h * HALF, (h + 1) * HALF)
-                nc.vector.tensor_tensor(r[:, c], num[b][:].indirect(half_of(bb_t, h)), part[:, c], MULT)
-            rate.append(r)
+        part = [pool.tile([P, S], F32, name="part%d" % b) for b in range(BLOCKS)]
+        rate = [pool.tile([P, S], F32, name="rate%d" % b) for b in range(BLOCKS)]
+        for h, c in enumerate(halves):
+            nc.vector.tensor_tensor(part[0][:, c], num0[:].indirect(half_of(ba_t, h)), kern_t[:, c], MULT)
+        for h, c in enumerate(halves):
+            nc.vector.tensor_tensor(rate[0][:, c], num0[:].indirect(half_of(bb_t, h)), part[0][:, c], MULT)
+        nc.vector.scalar_tensor_tensor(part[1][:], ea[:], 1.0 / 25.0, kern_t[:], MULT, MULT)
+        inv = [pool.tile([P, V], F32, name="inv0", tag="ea"), pool.tile([P, V], F32, name="inv1")]
+        for b, z in enumerate((z0, z1)):
+            nc.scalar.activation(inv[b][:], z[:].indirect(who_t[:]), ACT.Sigmoid)
         first = [pool.tile([P, V], F32, name="first%d" % b) for b in range(BLOCKS)]
         both = [pool.tile([P, V], F32, name="both%d" % b) for b in range(BLOCKS)]
         loss = [pool.tile([P, V], F32, name="loss%d" % b) for b in range(BLOCKS)]
         logg = [pool.tile([P, V], F32, name="logg%d" % b) for b in range(BLOCKS)]
         res = [pool.tile([P, V], F32, name="res%d" % b) for b in range(BLOCKS)]
+        nc.vector.tensor_copy(first[0][:], rate[0][:].indirect(gaina_t[:]))
+        nc.vector.tensor_tensor(rate[1][:], part[1][:], eb[:], MULT)
+        nc.vector.tensor_tensor(both[0][:], rate[0][:].indirect(gainb_t[:]), first[0][:], ADD)
+        nc.vector.tensor_copy(first[1][:], rate[1][:].indirect(gaina_t[:]))
+        nc.vector.tensor_tensor(loss[0][:], rate[0][:].indirect(lossa_t[:]), inv[0][:], MULT)
+        nc.vector.tensor_tensor(both[1][:], rate[1][:].indirect(gainb_t[:]), first[1][:], ADD)
+        nc.vector.tensor_tensor(loss[1][:], rate[1][:].indirect(lossa_t[:]), inv[1][:], MULT)
         for b in range(BLOCKS):
-            nc.vector.tensor_copy(first[b][:], rate[b][:].indirect(gaina_t[:]))
-        for b in range(BLOCKS):
-            nc.vector.tensor_tensor(both[b][:], rate[b][:].indirect(gainb_t[:]), first[b][:], ADD)
             nc.scalar.activation(logg[b][:], both[b][:], ACT.Ln, scale=0.5, bias=0.1)
-        for b in range(BLOCKS):
-            nc.vector.tensor_tensor(loss[b][:], rate[b][:].indirect(lossa_t[:]), inv[b][:], MULT)
-        for b in range(BLOCKS):
             nc.vector.scalar_tensor_tensor(res[b][:], loss[b][:], loss_w[:, b:b + 1], logg[b][:], MULT, ADD)
             nc.sync.dma_start(out[b * P:(b + 1) * P, :], res[b][:])

import math
from contextlib import ExitStack

import concourse.mybir as mybir

K, T, S, N, V = 1024, 1024, 512, 256, 256
FLOPS = 2 * K * N * S

F32 = mybir.dt.float32
BF16 = mybir.dt.bfloat16
I32 = mybir.dt.int32
U32 = mybir.dt.uint32
U16 = mybir.dt.uint16
U8 = mybir.dt.uint8
FP8X4 = mybir.dt.float8_e4m3fn_x4
ACT = mybir.ActivationFunctionType
MULT = mybir.AluOpType.mult
ADD = mybir.AluOpType.add

P = 128
PACK = 4
PASSES = K // (P * PACK)
BLOCKS = N // P
HALF = S // 2
LIST_ROWS = 16
EXP_WINDOW = 2048


def tile_picked_ycoagu_log_p_kernel(tc, x_words, x_scales, w1, kern, sink, offs, ba, bb, gaina, gainb, lossa, who, out):
    nc = tc.nc
    with ExitStack() as ctx:
        pool = ctx.enter_context(tc.tile_pool(name="sbuf", bufs=1))
        psum = ctx.enter_context(tc.psum_pool(name="psum", bufs=1))

        def load_list(name, src):
            t = pool.tile(list(src.shape), U16, name=name)
            nc.sync.dma_start(t[:], src)
            return t

        def half_of(lst, h):
            cols = HALF // LIST_ROWS
            return lst[:, h * cols:(h + 1) * cols]

        w_view = w1.rearrange("(o p t) n -> o p t n", p=P, t=PACK)

        def load_w(name, o, cols):
            t = pool.tile([P, PACK, cols.stop - cols.start], F32, name=name)
            nc.sync.dma_start(t[:], w_view[o][:, :, cols])
            return t

        def load_x(o):
            t = pool.tile([P, T], I32, name="xw%d" % o)
            nc.sync.dma_start(t[:], x_words[o].rearrange("p n t -> p (n t)").bitcast(I32))
            return t

        w_raw = [load_w("w_raw0", 0, slice(0, N))]
        offs_t = load_list("offs_t", offs)
        xs = pool.tile([P, T], U8, name="xs")
        nc.gpsimd.memset(xs[:].bitcast(I32), 0)
        for q in range(4):
            nc.sync.dma_start(xs[32 * q:32 * q + 4 * PASSES, :].bitcast(I32), x_scales[:, 4 * q:4 * q + 4, :].bitcast(I32))
        w_raw.append(load_w("w_raw1", 1, slice(0, N)))
        xw = [load_x(o) for o in range(PASSES)]
        ba_t = load_list("ba_t", ba)
        bb_t = load_list("bb_t", bb)
        kern_t = pool.tile([P, S], F32, name="kern_t")
        nc.sync.dma_start(kern_t[:], kern)
        who_t = load_list("who_t", who)
        gaina_t = load_list("gaina_t", gaina)
        gainb_t = load_list("gainb_t", gainb)
        lossa_t = load_list("lossa_t", lossa)
        sink_t = pool.tile([P, BLOCKS], F32, name="sink_t")
        with nc.allow_non_contiguous_dma(reason="one value a row"):
            nc.sync.dma_start(sink_t[:], sink.rearrange("(b p) o -> p (b o)", p=P))
        loss_w = pool.tile([P, BLOCKS], F32, name="loss_w")
        nc.gpsimd.tensor_scalar(loss_w[:], sink_t[:], -5.0, 0.0, MULT, ADD)

        def quantize_w(name, raw, copy):
            width = raw.shape[2]
            grouped = pool.tile([P, width * PACK], BF16, name=name + "_grouped", tag=name + "_stage", align_bytes=64)
            copy(grouped[:].rearrange("p (c i t) -> p c t i", i=4, t=PACK),
                 raw[:].rearrange("p t (c i) -> p c t i", i=4))
            codes = pool.tile([P, width], U32, name=name + "_codes", align_bytes=64)
            scales = pool.tile([P, width], U8, name=name + "_scales", align_bytes=64)
            nc.vector.quantize_mx(out=codes[:].bitcast(FP8X4), scales=scales[:], in_=grouped[:])
            return codes, scales

        xs_g = pool.tile([P, S], U8, name="xs_g", align_bytes=64)
        xw_g0 = pool.tile([P, S], U32, name="xw_g0", align_bytes=64)
        nc.vector.tensor_copy(xs_g[:], xs[:].indirect(offs_t[:]))
        wq = [quantize_w("w%d" % o, w_raw[o], nc.scalar.copy) for o in range(PASSES)]
        nc.vector.tensor_copy(xw_g0[:], xw[0][:].bitcast(U32).indirect(offs_t[:]))
        xw_g1 = []
        for h, stage in enumerate(("w1_stage", "w0_stage")):
            t = pool.tile([P, HALF], U32, name="xw_g1_%d" % h, tag=stage, align_bytes=64)
            nc.vector.tensor_copy(t[:], xw[1][:].bitcast(U32).indirect(half_of(offs_t, h)))
            xw_g1.append(t)

        halves = [slice(0, HALF), slice(HALF, S)]
        y = [[psum.tile([P, HALF], F32, name="y%d_%d" % (b, h)) for h in range(2)] for b in range(BLOCKS)]
        for o in range(PASSES):
            codes, scales = wq[o]
            for h, cols in enumerate(halves):
                words = xw_g0[:, cols] if o == 0 else xw_g1[h][:]
                for b in range(BLOCKS):
                    nc.tensor.matmul_mx(
                        out=y[b][h][:],
                        lhsT=codes[:, b * P:(b + 1) * P].bitcast(FP8X4),
                        lhsT_scale=scales[:, b * P:(b + 1) * P],
                        rhs=words.bitcast(FP8X4),
                        rhs_scale=xs_g[4 * o:, cols],
                        start=(o == 0), stop=(o == PASSES - 1))
        num0 = pool.tile([P, S], F32, name="num0")
        z0 = pool.tile([P, S], F32, name="z0")
        z1 = pool.tile([P, EXP_WINDOW], F32, name="z1")
        nc.vector.memset(z1[:, S:], 0.0)
        for h, c in enumerate(halves):
            nc.scalar.activation(num0[:, c], y[0][h][:], ACT.Exp, scale=0.6)
            nc.scalar.activation(z1[:, c], y[1][h][:], ACT.Copy, scale=-0.6, bias=-math.log(5.0))
            nc.vector.tensor_scalar(z0[:, c], y[0][h][:], -0.6, -math.log(5.0), MULT, ADD)
        ea = pool.tile([P, S], F32, name="ea", tag="ea")
        eb = pool.tile([P, S], F32, name="eb")
        nc.scalar.activation(ea[:], z1[:].indirect(ba_t[:]), ACT.Exp, scale=-1.0)
        nc.scalar.activation(eb[:], z1[:].indirect(bb_t[:]), ACT.Exp, scale=-1.0)

        part = [pool.tile([P, S], F32, name="part%d" % b) for b in range(BLOCKS)]
        rate = [pool.tile([P, S], F32, name="rate%d" % b) for b in range(BLOCKS)]
        for h, c in enumerate(halves):
            nc.vector.tensor_tensor(part[0][:, c], num0[:].indirect(half_of(ba_t, h)), kern_t[:, c], MULT)
        for h, c in enumerate(halves):
            nc.vector.tensor_tensor(rate[0][:, c], num0[:].indirect(half_of(bb_t, h)), part[0][:, c], MULT)
        nc.vector.scalar_tensor_tensor(part[1][:], ea[:], 1.0 / 25.0, kern_t[:], MULT, MULT)
        inv = [pool.tile([P, V], F32, name="inv0", tag="ea"), pool.tile([P, V], F32, name="inv1")]
        for b, z in enumerate((z0, z1)):
            nc.scalar.activation(inv[b][:], z[:].indirect(who_t[:]), ACT.Sigmoid)
        first = [pool.tile([P, V], F32, name="first%d" % b) for b in range(BLOCKS)]
        both = [pool.tile([P, V], F32, name="both%d" % b) for b in range(BLOCKS)]
        loss = [pool.tile([P, V], F32, name="loss%d" % b) for b in range(BLOCKS)]
        logg = [pool.tile([P, V], F32, name="logg%d" % b) for b in range(BLOCKS)]
        res = [pool.tile([P, V], F32, name="res%d" % b) for b in range(BLOCKS)]
        nc.vector.tensor_copy(first[0][:], rate[0][:].indirect(gaina_t[:]))
        nc.vector.tensor_tensor(rate[1][:], part[1][:], eb[:], MULT)
        nc.vector.tensor_tensor(both[0][:], rate[0][:].indirect(gainb_t[:]), first[0][:], ADD)
        nc.vector.tensor_copy(first[1][:], rate[1][:].indirect(gaina_t[:]))
        nc.vector.tensor_tensor(loss[0][:], rate[0][:].indirect(lossa_t[:]), inv[0][:], MULT)
        nc.vector.tensor_tensor(both[1][:], rate[1][:].indirect(gainb_t[:]), first[1][:], ADD)
        nc.vector.tensor_tensor(loss[1][:], rate[1][:].indirect(lossa_t[:]), inv[1][:], MULT)
        for b in range(BLOCKS):
            nc.scalar.activation(logg[b][:], both[b][:], ACT.Ln, scale=0.5, bias=0.1)
            nc.vector.scalar_tensor_tensor(res[b][:], loss[b][:], loss_w[:, b:b + 1], logg[b][:], MULT, ADD)
            nc.sync.dma_start(out[b * P:(b + 1) * P, :], res[b][:])
